import numpy as np, ml_dtypes
CORES = [1,5,73,77,129,133,201,205]
N = 8
KB, QP = 1, 128
def setup_inputs(rng):
    return {"q": rng.standard_normal((N, 128, QP), dtype=np.float32).astype(ml_dtypes.bfloat16), "k": rng.standard_normal((N, 128, KB * 128), dtype=np.float32).astype(ml_dtypes.bfloat16), "v": rng.standard_normal((N, 128, KB * 128), dtype=np.float32).astype(ml_dtypes.bfloat16)}
def reference(q, k, v):
    Q, K, V = q.astype(np.float64), k.astype(np.float64), v.astype(np.float64)
    y = np.zeros((N, 128, QP))
    for r in range(N):
        for j in range(r + 1):
            for b in range(KB):
                S = np.maximum(K[j][:, 128 * b:128 * b + 128].T @ Q[r], 0.0)
                y[r] += V[j][:, 128 * b:128 * b + 128].T @ S
    return {"y": y.astype(ml_dtypes.bfloat16 if q.dtype != np.float64 else np.float64)}

@@ -1,0 +1,211 @@
+from concourse.bass import DstId, RemoteDMATransfer
+from concourse.mybir import AluOpType
+
+ROUTE = {(0, 1): "Y", (0, 3): "X", (1, 2): "X", (2, 3): "Y"}
+NT = 6
+
+SCRATCH = {
+    "dk": ("dram", [128, 128], "bfloat16"),
+    "dv": ("dram", [128, 128], "bfloat16"),
+    "kv": ("sbuf", [128, 256], "bfloat16"),
+    "qq": ("sbuf", [128, 256], "bfloat16"),
+    "land": ("sbuf", [128, 768], "bfloat16"),
+    "zero": ("sbuf", [128, 256], "float32"),
+    "ssb": ("sbuf", [128, 1024], "bfloat16"),
+    "opsb": ("sbuf", [128, 128], "bfloat16"),
+    "oland": ("sbuf", [128, 128], "bfloat16"),
+    "ysb": ("sbuf", [128, 128], "bfloat16"),
+    "pe": ("psum", [128, 512], "float32"),
+    "pl0": ("psum", [128, 512], "float32"),
+    "pl1": ("psum", [128, 512], "float32"),
+    "pop": ("psum", [128, 512], "float32"),
+    "pown": ("psum", [128, 512], "float32"),
+}
+SEMAPHORES = (["ld_d", "ld_kv", "ld_q", "qarr", "harr", "sent", "zs", "opd", "owd", "opc", "oarr", "yd", "st"]
+              + ["ka%d" % i for i in range(3)] + ["va%d" % i for i in range(3)]
+              + ["sd%d" % i for i in range(NT)] + ["rd%d" % i for i in range(NT)])
+
+
+def _bits(m):
+    return bin(m).count("1")
+
+
+def _first_hops(j, cores):
+    cj = j // 2
+    on, off = [], []
+    for cd in range(cj + 1, 4):
+        if (cd - cj) % 2 == 0:
+            continue
+        d = 2 * cd + j % 2
+        x = ROUTE[(cj, cd)] == "X"
+        base = (cores[j] - cores[j] % 8) if x else ((cores[d] - cores[d] % 8) ^ 8)
+        h = base + (2 if j % 2 == 0 else 6)
+        (on if x else off).extend([(h, 0, d), (h + 1, 1, d)])
+    out = []
+    if off:
+        per = 8 // len(off)
+        for i, e in enumerate(off):
+            out.append(e + ((((1 << per) - 1) << (i * per)),))
+    if on:
+        lo, pool = (8, 8) if off else (0, 16)
+        per = pool // len(on)
+        for i, e in enumerate(on):
+            out.append(e + ((((1 << per) - 1) << (lo + i * per)),))
+    return out
+
+
+def rank_program(g, core, T, topo):
+    cores = T.cores
+    sem = T.sem
+    r = T.rank_of(core)
+
+    if r is None:
+        for j in range(6):
+            for (h, half, d, m) in _first_hops(j, cores):
+                if h != core:
+                    continue
+                rid, pid = topo.addr(cores[d], core)
+                c0 = (j // 2) * 256 + half * 128
+                g.wait_ge(sem.harr, _bits(m))
+                g.remote_dma(out_ap=T.land[:, c0:c0 + 128], in_ap=T.dk[:, :],
+                             remote_sem=sem[("va%d" if half else "ka%d") % (j // 2)], local_sem=sem.sent,
+                             pid=pid, routing_id=rid, dma_engine_mask=0x00FF)
+                g.wait_ge(sem.sent, 8)
+        return
+
+    c, par = r // 2, r % 2
+    hops = _first_hops(r, cores) if r < 6 else []
+    swap = c >= 1
+
+    if hops:
+        g.sync.dma_start(T.dk[:, :], T.k[:, :]).then_inc(sem.ld_d, 16)
+        g.scalar.dma_start(T.dv[:, :], T.v[:, :]).then_inc(sem.ld_d, 16)
+        g.sync.dma_start(T.kv[:, 0:128], T.k[:, :]).then_inc(sem.ld_kv, 16)
+        g.scalar.dma_start(T.kv[:, 128:256], T.v[:, :]).then_inc(sem.ld_kv, 16)
+        g.sync.dma_start(T.qq[:, 128:256], T.q[:, :]).then_inc(sem.ld_q, 16)
+    else:
+        g.sync.dma_start(T.qq[:, 128:256], T.q[:, :]).then_inc(sem.ld_q, 16)
+        g.scalar.dma_start(T.kv[:, 128:256], T.v[:, :]).then_inc(sem.ld_kv, 16)
+        g.sync.dma_start(T.kv[:, 0:128], T.k[:, :]).then_inc(sem.ld_kv, 16)
+
+    if not swap:
+        early = [(r, "w")] + ([(0, "w")] if r == 1 else [])
+        late = []
+    else:
+        early = [(r, "pw" if par == 0 else "w")] + ([(r - 4, "pw")] if c >= 2 else [])
+        late = [r - 2] + ([r - 6] if c == 3 else [])
+    spec = [(j, kind, "pe") for (j, kind) in early]
+    spec += [(j, "p", "pl%d" % i) for i, j in enumerate(late)]
+    spec += [(j, "w", "pl%d" % i) for i, j in enumerate(late)]
+    offs, o = [], 0
+    for (j, kind, bank) in spec:
+        offs.append(o)
+        o += 128 * len(kind)
+    ne, nl = len(early), len(late)
+
+    def block(j):
+        if j == r:
+            return T.kv[:, 0:128], T.kv[:, 128:256], ("ld_kv", 32), ("ld_kv", 32)
+        s = j // 2
+        ka, va = T.land[:, s * 256:s * 256 + 128], T.land[:, s * 256 + 128:s * 256 + 256]
+        if j // 2 == c:
+            return ka, va, ("ka%d" % s, 16), ("ka%d" % s, 16)
+        if (c - j // 2) % 2 == 0:
+            return ka, va, ("ka%d" % s, 8), ("ka%d" % s, 8)
+        return ka, va, ("ka%d" % s, 8), ("va%d" % s, 8)
+
+    nsent = 0
+    if hops:
+        g.wait_ge(sem.ld_d, 32)
+        trs = []
+        for (h, half, d, m) in hops:
+            rid, pid = topo.addr(h, core)
+            trs.append(RemoteDMATransfer(dst_ids=[DstId(rid=rid, pnc=pid)], dma_engine_mask=m, remote_sem=sem.harr,
+                                         src=(T.dv if half else T.dk)[:, :], dst=T.dk[:, :]))
+            nsent += _bits(m)
+        g.remote_dma_fused(trs, local_sem=sem.sent)
+    if r < 4:
+        rid, pid = topo.addr(cores[r + 4], core)
+        g.wait_ge(sem.ld_kv, 32)
+        g.remote_dma(out_ap=T.land[:, c * 256:c * 256 + 256], in_ap=T.kv[:, :], remote_sem=sem["ka%d" % c],
+                     local_sem=sem.sent, pid=pid, routing_id=rid, dma_engine_mask=0x00FF)
+        nsent += 8
+    prid, ppid = topo.addr(cores[r ^ 1], core)
+    if r == 0:
+        g.remote_dma(out_ap=T.land[:, 0:256], in_ap=T.kv[:, :], remote_sem=sem.ka0, local_sem=sem.sent,
+                     pid=ppid, routing_id=prid, dma_engine_mask=0xFFFF)
+        nsent += 16
+    if swap:
+        g.wait_ge(sem.ld_q, 16)
+        g.remote_dma(out_ap=T.qq[:, 0:128], in_ap=T.qq[:, 128:256], remote_sem=sem.qarr, local_sem=sem.sent,
+                     pid=ppid, routing_id=prid, dma_engine_mask=0xFFFF)
+        g.wait_ge(sem.opc, 1)
+        g.remote_dma(out_ap=T.oland[:, :], in_ap=T.opsb[:, :], remote_sem=sem.oarr, local_sem=sem.sent,
+                     pid=ppid, routing_id=prid, dma_engine_mask=0xFFFF)
+        nsent += 32
+    if nsent:
+        g.wait_ge(sem.sent, nsent)
+
+    order = []
+    for t in range(ne):
+        order.append(("S", t, ""))
+        for grp in spec[t][1]:
+            order.append(("O", t, grp))
+    for (lo, grp) in ((ne, "p"), (ne + nl, "w")):
+        for t in range(lo, lo + nl):
+            order.append(("S", t, ""))
+        for t in range(lo, lo + nl):
+            order.append(("O", t, grp))
+    first, last = {}, {}
+    for i, (op, t, grp) in enumerate(order):
+        if op == "O":
+            first.setdefault(grp, i)
+            last[grp] = i
+    waited = set()
+
+    def twait(name, val):
+        if (name, val) not in waited:
+            waited.add((name, val))
+            g.tensor.wait_ge(sem[name], val)
+
+    for i, (op, t, grp) in enumerate(order):
+        j, kind, bank = spec[t]
+        ka, va, kready, vready = block(j)
+        n = 128 * len(kind)
+        if op == "S":
+            if "p" in kind:
+                twait("qarr", 16)
+            if "w" in kind:
+                twait("ld_q", 16)
+            twait(kready[0], kready[1])
+            q0 = 0 if "p" in kind else 128
+            g.tensor.matmul(T[bank][:, 0:n], ka, T.qq[:, q0:q0 + n], True, True).then_inc(sem["sd%d" % t], 1)
+        else:
+            twait("rd%d" % t, 1)
+            twait(vready[0], vready[1])
+            s0 = offs[t] + (128 if (kind == "pw" and grp == "w") else 0)
+            acc = T.pop if grp == "p" else T.pown
+            mm = g.tensor.matmul(acc[:, 0:128], va, T.ssb[:, s0:s0 + 128], i == first[grp], i == last[grp])
+            if i == last[grp]:
+                mm.then_inc(sem.opd if grp == "p" else sem.owd, 1)
+
+    g.vector.memset(T.zero[:, :], 0.0).then_inc(sem.zs, 1)
+    g.vector.wait_ge(sem.zs, 1)
+    for t, (j, kind, bank) in enumerate(spec):
+        if swap and t == ne + nl:
+            g.vector.wait_ge(sem.opd, 1)
+            g.vector.tensor_copy(T.opsb[:, :], T.pop[:, 0:128]).then_inc(sem.opc, 1)
+        n = 128 * len(kind)
+        g.vector.wait_ge(sem["sd%d" % t], 1)
+        g.vector.tensor_tensor(T.ssb[:, offs[t]:offs[t] + n], T[bank][:, 0:n], T.zero[:, 0:n],
+                               AluOpType.max).then_inc(sem["rd%d" % t], 1)
+    g.vector.wait_ge(sem.owd, 1)
+    if swap:
+        g.vector.wait_ge(sem.oarr, 16)
+        g.vector.tensor_tensor(T.ysb[:, :], T.pown[:, 0:128], T.oland[:, :], AluOpType.add).then_inc(sem.yd, 1)
+    else:
+        g.vector.tensor_copy(T.ysb[:, :], T.pown[:, 0:128]).then_inc(sem.yd, 1)
+
+    g.sync.wait_ge(sem.yd, 1)
+    g.sync.dma_start(T.y[:, :], T.ysb[:, :]).then_inc(sem.st, 16)
+    g.sync.wait_ge(sem.st, 16)

@@ -2,28 +2,26 @@ from concourse.bass import DstId, RemoteDMATransfer
 from concourse.mybir import AluOpType
 
 ROUTE = {(0, 1): "Y", (0, 3): "X", (1, 2): "X", (2, 3): "Y"}
-NT = 6
+NB = 4
 
 SCRATCH = {
     "dk": ("dram", [128, 128], "bfloat16"),
     "dv": ("dram", [128, 128], "bfloat16"),
     "kv": ("sbuf", [128, 256], "bfloat16"),
-    "qq": ("sbuf", [128, 256], "bfloat16"),
-    "land": ("sbuf", [128, 768], "bfloat16"),
-    "zero": ("sbuf", [128, 256], "float32"),
+    "qs": ("sbuf", [128, 128], "bfloat16"),
+    "land": ("sbuf", [128, 7 * 256], "bfloat16"),
+    "zero": ("sbuf", [128, 128], "float32"),
     "ssb": ("sbuf", [128, 1024], "bfloat16"),
-    "opsb": ("sbuf", [128, 128], "bfloat16"),
-    "oland": ("sbuf", [128, 128], "bfloat16"),
     "ysb": ("sbuf", [128, 128], "bfloat16"),
-    "pe": ("psum", [128, 512], "float32"),
-    "pl0": ("psum", [128, 512], "float32"),
-    "pl1": ("psum", [128, 512], "float32"),
-    "pop": ("psum", [128, 512], "float32"),
+    "ps0": ("psum", [128, 512], "float32"),
+    "ps1": ("psum", [128, 512], "float32"),
+    "ps2": ("psum", [128, 512], "float32"),
+    "ps3": ("psum", [128, 512], "float32"),
     "pown": ("psum", [128, 512], "float32"),
 }
-SEMAPHORES = (["ld_d", "ld_kv", "ld_q", "qarr", "harr", "sent", "zs", "opd", "owd", "opc", "oarr", "yd", "st"]
-              + ["ka%d" % i for i in range(3)] + ["va%d" % i for i in range(3)]
-              + ["sd%d" % i for i in range(NT)] + ["rd%d" % i for i in range(NT)])
+SEMAPHORES = (["ld_d", "ld_kv", "ld_q", "harr", "sent", "zs", "owd", "yd", "st"]
+              + ["ka%d" % i for i in range(7)] + ["va%d" % i for i in range(7)]
+              + ["sd%d" % i for i in range(8)] + ["rd%d" % i for i in range(8)])
 
 
 def _bits(m):
@@ -36,11 +34,11 @@ def _first_hops(j, cores):
     for cd in range(cj + 1, 4):
         if (cd - cj) % 2 == 0:
             continue
-        d = 2 * cd + j % 2
+        d = 2 * cd
         x = ROUTE[(cj, cd)] == "X"
         base = (cores[j] - cores[j] % 8) if x else ((cores[d] - cores[d] % 8) ^ 8)
         h = base + (2 if j % 2 == 0 else 6)
-        (on if x else off).extend([(h, 0, d), (h + 1, 1, d)])
+        (on if x else off).extend([(h, 0, cd), (h + 1, 1, cd)])
     out = []
     if off:
         per = 8 // len(off)
@@ -61,150 +59,103 @@ def rank_program(g, core, T, topo):
 
     if r is None:
         for j in range(6):
-            for (h, half, d, m) in _first_hops(j, cores):
+            for (h, half, cd, m) in _first_hops(j, cores):
                 if h != core:
                     continue
-                rid, pid = topo.addr(cores[d], core)
-                c0 = (j // 2) * 256 + half * 128
+                c0 = j * 256 + half * 128
+                trs = []
+                for i in range(2):
+                    rid, pid = topo.addr(cores[2 * cd + i], core)
+                    trs.append(RemoteDMATransfer(dst_ids=[DstId(rid=rid, pnc=pid)], dma_engine_mask=0x0F << (4 * i),
+                                                 remote_sem=sem[("va%d" if half else "ka%d") % j],
+                                                 src=T.dk[:, :], dst=T.land[:, c0:c0 + 128]))
                 g.wait_ge(sem.harr, _bits(m))
-                g.remote_dma(out_ap=T.land[:, c0:c0 + 128], in_ap=T.dk[:, :],
-                             remote_sem=sem[("va%d" if half else "ka%d") % (j // 2)], local_sem=sem.sent,
-                             pid=pid, routing_id=rid, dma_engine_mask=0x00FF)
+                g.remote_dma_fused(trs, local_sem=sem.sent)
                 g.wait_ge(sem.sent, 8)
         return
 
     c, par = r // 2, r % 2
     hops = _first_hops(r, cores) if r < 6 else []
-    swap = c >= 1
 
     if hops:
         g.sync.dma_start(T.dk[:, :], T.k[:, :]).then_inc(sem.ld_d, 16)
         g.scalar.dma_start(T.dv[:, :], T.v[:, :]).then_inc(sem.ld_d, 16)
-        g.sync.dma_start(T.kv[:, 0:128], T.k[:, :]).then_inc(sem.ld_kv, 16)
-        g.scalar.dma_start(T.kv[:, 128:256], T.v[:, :]).then_inc(sem.ld_kv, 16)
-        g.sync.dma_start(T.qq[:, 128:256], T.q[:, :]).then_inc(sem.ld_q, 16)
-    else:
-        g.sync.dma_start(T.qq[:, 128:256], T.q[:, :]).then_inc(sem.ld_q, 16)
-        g.scalar.dma_start(T.kv[:, 128:256], T.v[:, :]).then_inc(sem.ld_kv, 16)
-        g.sync.dma_start(T.kv[:, 0:128], T.k[:, :]).then_inc(sem.ld_kv, 16)
+    g.sync.dma_start(T.kv[:, 0:128], T.k[:, :]).then_inc(sem.ld_kv, 16)
+    g.scalar.dma_start(T.kv[:, 128:256], T.v[:, :]).then_inc(sem.ld_kv, 16)
+    g.sync.dma_start(T.qs[:, :], T.q[:, :]).then_inc(sem.ld_q, 16)
 
-    if not swap:
-        early = [(r, "w")] + ([(0, "w")] if r == 1 else [])
-        late = []
-    else:
-        early = [(r, "pw" if par == 0 else "w")] + ([(r - 4, "pw")] if c >= 2 else [])
-        late = [r - 2] + ([r - 6] if c == 3 else [])
-    spec = [(j, kind, "pe") for (j, kind) in early]
-    spec += [(j, "p", "pl%d" % i) for i, j in enumerate(late)]
-    spec += [(j, "w", "pl%d" % i) for i, j in enumerate(late)]
-    offs, o = [], 0
-    for (j, kind, bank) in spec:
-        offs.append(o)
-        o += 128 * len(kind)
-    ne, nl = len(early), len(late)
+    js = [r] + ([r - 1] if par else [])
+    if c >= 2:
+        js += [2 * (c - 2), 2 * (c - 2) + 1]
+    if c >= 1:
+        js += [2 * (c - 1), 2 * (c - 1) + 1]
+    if c == 3:
+        js += [0, 1]
+    n = len(js)
 
     def block(j):
         if j == r:
             return T.kv[:, 0:128], T.kv[:, 128:256], ("ld_kv", 32), ("ld_kv", 32)
-        s = j // 2
-        ka, va = T.land[:, s * 256:s * 256 + 128], T.land[:, s * 256 + 128:s * 256 + 256]
+        ka, va = T.land[:, j * 256:j * 256 + 128], T.land[:, j * 256 + 128:j * 256 + 256]
         if j // 2 == c:
-            return ka, va, ("ka%d" % s, 16), ("ka%d" % s, 16)
+            return ka, va, ("ka%d" % j, 16), ("ka%d" % j, 16)
         if (c - j // 2) % 2 == 0:
-            return ka, va, ("ka%d" % s, 8), ("ka%d" % s, 8)
-        return ka, va, ("ka%d" % s, 8), ("va%d" % s, 8)
+            return ka, va, ("ka%d" % j, 4), ("ka%d" % j, 4)
+        return ka, va, ("ka%d" % j, 4), ("va%d" % j, 4)
 
     nsent = 0
     if hops:
         g.wait_ge(sem.ld_d, 32)
         trs = []
-        for (h, half, d, m) in hops:
+        for (h, half, cd, m) in hops:
             rid, pid = topo.addr(h, core)
             trs.append(RemoteDMATransfer(dst_ids=[DstId(rid=rid, pnc=pid)], dma_engine_mask=m, remote_sem=sem.harr,
                                          src=(T.dv if half else T.dk)[:, :], dst=T.dk[:, :]))
             nsent += _bits(m)
         g.remote_dma_fused(trs, local_sem=sem.sent)
-    if r < 4:
-        rid, pid = topo.addr(cores[r + 4], core)
+    if r < 4 or par == 0:
         g.wait_ge(sem.ld_kv, 32)
-        g.remote_dma(out_ap=T.land[:, c * 256:c * 256 + 256], in_ap=T.kv[:, :], remote_sem=sem["ka%d" % c],
-                     local_sem=sem.sent, pid=pid, routing_id=rid, dma_engine_mask=0x00FF)
+    if r < 4:
+        trs = []
+        for i in range(2):
+            rid, pid = topo.addr(cores[2 * (c + 2) + i], core)
+            trs.append(RemoteDMATransfer(dst_ids=[DstId(rid=rid, pnc=pid)], dma_engine_mask=0x0F << (4 * i),
+                                         remote_sem=sem["ka%d" % r], src=T.kv[:, :],
+                                         dst=T.land[:, r * 256:r * 256 + 256]))
+        g.remote_dma_fused(trs, local_sem=sem.sent)
         nsent += 8
-    prid, ppid = topo.addr(cores[r ^ 1], core)
-    if r == 0:
-        g.remote_dma(out_ap=T.land[:, 0:256], in_ap=T.kv[:, :], remote_sem=sem.ka0, local_sem=sem.sent,
-                     pid=ppid, routing_id=prid, dma_engine_mask=0xFFFF)
+    if par == 0:
+        rid, pid = topo.addr(cores[r + 1], core)
+        g.remote_dma(out_ap=T.land[:, r * 256:r * 256 + 256], in_ap=T.kv[:, :], remote_sem=sem["ka%d" % r],
+                     local_sem=sem.sent, pid=pid, routing_id=rid, dma_engine_mask=0xFFFF)
         nsent += 16
-    if swap:
-        g.wait_ge(sem.ld_q, 16)
-        g.remote_dma(out_ap=T.qq[:, 0:128], in_ap=T.qq[:, 128:256], remote_sem=sem.qarr, local_sem=sem.sent,
-                     pid=ppid, routing_id=prid, dma_engine_mask=0xFFFF)
-        g.wait_ge(sem.opc, 1)
-        g.remote_dma(out_ap=T.oland[:, :], in_ap=T.opsb[:, :], remote_sem=sem.oarr, local_sem=sem.sent,
-                     pid=ppid, routing_id=prid, dma_engine_mask=0xFFFF)
-        nsent += 32
     if nsent:
         g.wait_ge(sem.sent, nsent)
 
-    order = []
-    for t in range(ne):
-        order.append(("S", t, ""))
-        for grp in spec[t][1]:
-            order.append(("O", t, grp))
-    for (lo, grp) in ((ne, "p"), (ne + nl, "w")):
-        for t in range(lo, lo + nl):
-            order.append(("S", t, ""))
-        for t in range(lo, lo + nl):
-            order.append(("O", t, grp))
-    first, last = {}, {}
-    for i, (op, t, grp) in enumerate(order):
-        if op == "O":
-            first.setdefault(grp, i)
-            last[grp] = i
-    waited = set()
-
-    def twait(name, val):
-        if (name, val) not in waited:
-            waited.add((name, val))
-            g.tensor.wait_ge(sem[name], val)
-
-    for i, (op, t, grp) in enumerate(order):
-        j, kind, bank = spec[t]
-        ka, va, kready, vready = block(j)
-        n = 128 * len(kind)
-        if op == "S":
-            if "p" in kind:
-                twait("qarr", 16)
-            if "w" in kind:
-                twait("ld_q", 16)
-            twait(kready[0], kready[1])
-            q0 = 0 if "p" in kind else 128
-            g.tensor.matmul(T[bank][:, 0:n], ka, T.qq[:, q0:q0 + n], True, True).then_inc(sem["sd%d" % t], 1)
-        else:
-            twait("rd%d" % t, 1)
-            twait(vready[0], vready[1])
-            s0 = offs[t] + (128 if (kind == "pw" and grp == "w") else 0)
-            acc = T.pop if grp == "p" else T.pown
-            mm = g.tensor.matmul(acc[:, 0:128], va, T.ssb[:, s0:s0 + 128], i == first[grp], i == last[grp])
-            if i == last[grp]:
-                mm.then_inc(sem.opd if grp == "p" else sem.owd, 1)
+    g.tensor.wait_ge(sem.ld_q, 16)
+    for t in range(n + 1):
+        if t < n:
+            ka, va, kready, vready = block(js[t])
+            g.tensor.wait_ge(sem[kready[0]], kready[1])
+            g.tensor.matmul(T["ps%d" % (t % NB)][:, 0:128], ka, T.qs[:, :], True, True).then_inc(sem["sd%d" % t], 1)
+        if t > 0:
+            u = t - 1
+            ka, va, kready, vready = block(js[u])
+            g.tensor.wait_ge(sem["rd%d" % u], 1)
+            if vready != kready:
+                g.tensor.wait_ge(sem[vready[0]], vready[1])
+            mm = g.tensor.matmul(T.pown[:, 0:128], va, T.ssb[:, u * 128:u * 128 + 128], u == 0, u == n - 1)
+            if u == n - 1:
+                mm.then_inc(sem.owd, 1)
 
     g.vector.memset(T.zero[:, :], 0.0).then_inc(sem.zs, 1)
     g.vector.wait_ge(sem.zs, 1)
-    for t, (j, kind, bank) in enumerate(spec):
-        if swap and t == ne + nl:
-            g.vector.wait_ge(sem.opd, 1)
-            g.vector.tensor_copy(T.opsb[:, :], T.pop[:, 0:128]).then_inc(sem.opc, 1)
-        n = 128 * len(kind)
+    for t in range(n):
         g.vector.wait_ge(sem["sd%d" % t], 1)
-        g.vector.tensor_tensor(T.ssb[:, offs[t]:offs[t] + n], T[bank][:, 0:n], T.zero[:, 0:n],
+        g.vector.tensor_tensor(T.ssb[:, t * 128:t * 128 + 128], T["ps%d" % (t % NB)][:, 0:128], T.zero[:, :],
                                AluOpType.max).then_inc(sem["rd%d" % t], 1)
     g.vector.wait_ge(sem.owd, 1)
-    if swap:
-        g.vector.wait_ge(sem.oarr, 16)
-        g.vector.tensor_tensor(T.ysb[:, :], T.pown[:, 0:128], T.oland[:, :], AluOpType.add).then_inc(sem.yd, 1)
-    else:
-        g.vector.tensor_copy(T.ysb[:, :], T.pown[:, 0:128]).then_inc(sem.yd, 1)
+    g.vector.tensor_copy(T.ysb[:, :], T.pown[:, 0:128]).then_inc(sem.yd, 1)
 
     g.sync.wait_ge(sem.yd, 1)
     g.sync.dma_start(T.y[:, :], T.ysb[:, :]).then_inc(sem.st, 16)

@@ -19,37 +19,29 @@ SCRATCH = {
     "ps3": ("psum", [128, 512], "float32"),
     "pown": ("psum", [128, 512], "float32"),
 }
-SEMAPHORES = (["ld_d", "ld_kv", "ld_q", "harr", "sent", "zs", "owd", "yd", "st"]
+SEMAPHORES = (["ld_d", "ld_kv", "ld_q", "harr", "harv", "sent", "zs", "owd", "yd", "st"]
               + ["ka%d" % i for i in range(7)] + ["va%d" % i for i in range(7)]
               + ["sd%d" % i for i in range(8)] + ["rd%d" % i for i in range(8)])
 
 
-def _bits(m):
-    return bin(m).count("1")
-
-
-def _first_hops(j, cores):
+def _routes(j, cores):
     cj = j // 2
-    on, off = [], []
+    pair = 2 if j % 2 == 0 else 6
+    cross, same = [], None
     for cd in range(cj + 1, 4):
+        there = cores[2 * cd] - cores[2 * cd] % 8
         if (cd - cj) % 2 == 0:
-            continue
-        d = 2 * cd
-        x = ROUTE[(cj, cd)] == "X"
-        base = (cores[j] - cores[j] % 8) if x else ((cores[d] - cores[d] % 8) ^ 8)
-        h = base + (2 if j % 2 == 0 else 6)
-        (on if x else off).extend([(h, 0, cd), (h + 1, 1, cd)])
-    out = []
-    if off:
-        per = 8 // len(off)
-        for i, e in enumerate(off):
-            out.append(e + ((((1 << per) - 1) << (i * per)),))
-    if on:
-        lo, pool = (8, 8) if off else (0, 16)
-        per = pool // len(on)
-        for i, e in enumerate(on):
-            out.append(e + ((((1 << per) - 1) << (lo + i * per)),))
-    return out
+            same = (there + pair, cd)
+        elif ROUTE[(cj, cd)] == "X":
+            cross.append((cores[j] - cores[j] % 8 + pair, cd, 8))
+        else:
+            cross.append(((there ^ 8) + pair, cd, 0))
+    return cross, same
+
+
+def _one(topo, core, d, mask, rsem, src, dst):
+    rid, pid = topo.addr(d, core)
+    return RemoteDMATransfer(dst_ids=[DstId(rid=rid, pnc=pid)], dma_engine_mask=mask, remote_sem=rsem, src=src, dst=dst)
 
 
 def rank_program(g, core, T, topo):
@@ -59,39 +51,48 @@ def rank_program(g, core, T, topo):
 
     if r is None:
         for j in range(6):
-            for (h, half, cd, m) in _first_hops(j, cores):
-                if h != core:
-                    continue
+            cross, same = _routes(j, cores)
+            for (h, cd, lo) in cross:
+                if core in (h, h + 1):
+                    rid, pid = topo.addr(cores[2 * cd + core - h], core)
+                    g.wait_ge(sem.harr, 4)
+                    g.remote_dma(out_ap=T.land[:, j * 256:j * 256 + 128], in_ap=T.dk[:, :], remote_sem=sem["ka%d" % j],
+                                 local_sem=sem.sent, pid=pid, routing_id=rid, dma_engine_mask=0x00FF)
+                    g.wait_ge(sem.harv, 4)
+                    g.remote_dma(out_ap=T.land[:, j * 256 + 128:j * 256 + 256], in_ap=T.dv[:, :],
+                                 remote_sem=sem["va%d" % j], local_sem=sem.sent, pid=pid, routing_id=rid,
+                                 dma_engine_mask=0x00FF)
+                    g.wait_ge(sem.sent, 16)
+            if same is not None and core in (same[0], same[0] + 1):
+                half = core - same[0]
                 c0 = j * 256 + half * 128
-                trs = []
-                for i in range(2):
-                    rid, pid = topo.addr(cores[2 * cd + i], core)
-                    trs.append(RemoteDMATransfer(dst_ids=[DstId(rid=rid, pnc=pid)], dma_engine_mask=0x0F << (4 * i),
-                                                 remote_sem=sem[("va%d" if half else "ka%d") % j],
-                                                 src=T.dk[:, :], dst=T.land[:, c0:c0 + 128]))
-                g.wait_ge(sem.harr, _bits(m))
+                trs = [_one(topo, core, cores[2 * same[1] + i], 0xFF << (8 * i), sem[("va%d" if half else "ka%d") % j],
+                            T.dk[:, :], T.land[:, c0:c0 + 128]) for i in range(2)]
+                g.wait_ge(sem.harr, 4)
                 g.remote_dma_fused(trs, local_sem=sem.sent)
-                g.wait_ge(sem.sent, 8)
+                g.wait_ge(sem.sent, 16)
         return
 
     c, par = r // 2, r % 2
-    hops = _first_hops(r, cores) if r < 6 else []
+    cross, same = _routes(r, cores)
 
-    if hops:
+    if cross:
         g.sync.dma_start(T.dk[:, :], T.k[:, :]).then_inc(sem.ld_d, 16)
         g.scalar.dma_start(T.dv[:, :], T.v[:, :]).then_inc(sem.ld_d, 16)
     g.sync.dma_start(T.kv[:, 0:128], T.k[:, :]).then_inc(sem.ld_kv, 16)
     g.scalar.dma_start(T.kv[:, 128:256], T.v[:, :]).then_inc(sem.ld_kv, 16)
     g.sync.dma_start(T.qs[:, :], T.q[:, :]).then_inc(sem.ld_q, 16)
 
-    js = [r] + ([r - 1] if par else [])
+    early = [r] + ([r - 1] if par else [])
     if c >= 2:
-        js += [2 * (c - 2), 2 * (c - 2) + 1]
+        early += [2 * (c - 2), 2 * (c - 2) + 1]
+    late = []
     if c >= 1:
-        js += [2 * (c - 1), 2 * (c - 1) + 1]
+        late += [2 * (c - 1), 2 * (c - 1) + 1]
     if c == 3:
-        js += [0, 1]
-    n = len(js)
+        late += [0, 1]
+    js = early + late
+    n, ne = len(js), len(early)
 
     def block(j):
         if j == r:
@@ -99,53 +100,55 @@ def rank_program(g, core, T, topo):
         ka, va = T.land[:, j * 256:j * 256 + 128], T.land[:, j * 256 + 128:j * 256 + 256]
         if j // 2 == c:
             return ka, va, ("ka%d" % j, 16), ("ka%d" % j, 16)
-        if (c - j // 2) % 2 == 0:
-            return ka, va, ("ka%d" % j, 4), ("ka%d" % j, 4)
-        return ka, va, ("ka%d" % j, 4), ("va%d" % j, 4)
+        return ka, va, ("ka%d" % j, 8), ("va%d" % j, 8)
 
     nsent = 0
-    if hops:
+    if cross:
+        kcall = [_one(topo, core, h + i, 0xF << (lo + 4 * i), sem.harr, T.dk[:, :], T.dk[:, :])
+                 for (h, cd, lo) in cross for i in range(2)]
+        vcall = [_one(topo, core, h + i, 0xF << (lo + 4 * i), sem.harv, T.dv[:, :], T.dv[:, :])
+                 for (h, cd, lo) in cross for i in range(2)]
+        scall = []
+        if same is not None:
+            scall = [_one(topo, core, same[0], 0x000F, sem.harr, T.dk[:, :], T.dk[:, :]),
+                     _one(topo, core, same[0] + 1, 0x00F0, sem.harr, T.dv[:, :], T.dk[:, :])]
+        if scall and all(lo == 8 for (h, cd, lo) in cross):
+            kcall, scall = kcall + scall, []
         g.wait_ge(sem.ld_d, 32)
-        trs = []
-        for (h, half, cd, m) in hops:
-            rid, pid = topo.addr(h, core)
-            trs.append(RemoteDMATransfer(dst_ids=[DstId(rid=rid, pnc=pid)], dma_engine_mask=m, remote_sem=sem.harr,
-                                         src=(T.dv if half else T.dk)[:, :], dst=T.dk[:, :]))
-            nsent += _bits(m)
-        g.remote_dma_fused(trs, local_sem=sem.sent)
-    if r < 4 or par == 0:
-        g.wait_ge(sem.ld_kv, 32)
-    if r < 4:
-        trs = []
-        for i in range(2):
-            rid, pid = topo.addr(cores[2 * (c + 2) + i], core)
-            trs.append(RemoteDMATransfer(dst_ids=[DstId(rid=rid, pnc=pid)], dma_engine_mask=0x0F << (4 * i),
-                                         remote_sem=sem["ka%d" % r], src=T.kv[:, :],
-                                         dst=T.land[:, r * 256:r * 256 + 256]))
-        g.remote_dma_fused(trs, local_sem=sem.sent)
-        nsent += 8
+        for call in (kcall, scall, vcall):
+            if call:
+                g.remote_dma_fused(call, local_sem=sem.sent)
+                nsent += 4 * len(call)
     if par == 0:
         rid, pid = topo.addr(cores[r + 1], core)
+        g.wait_ge(sem.ld_kv, 32)
         g.remote_dma(out_ap=T.land[:, r * 256:r * 256 + 256], in_ap=T.kv[:, :], remote_sem=sem["ka%d" % r],
                      local_sem=sem.sent, pid=pid, routing_id=rid, dma_engine_mask=0xFFFF)
         nsent += 16
     if nsent:
         g.wait_ge(sem.sent, nsent)
 
+    order = []
+    for t in range(ne):
+        order.append(("S", t))
+        if t > 0:
+            order.append(("O", t - 1))
+    if late:
+        order.append(("S", ne))
+    order.append(("O", ne - 1))
+    order += [("S", t) for t in range(ne + 1, n)] + [("O", t) for t in range(ne, n)]
     g.tensor.wait_ge(sem.ld_q, 16)
-    for t in range(n + 1):
-        if t < n:
-            ka, va, kready, vready = block(js[t])
+    for (op, t) in order:
+        ka, va, kready, vready = block(js[t])
+        if op == "S":
             g.tensor.wait_ge(sem[kready[0]], kready[1])
             g.tensor.matmul(T["ps%d" % (t % NB)][:, 0:128], ka, T.qs[:, :], True, True).then_inc(sem["sd%d" % t], 1)
-        if t > 0:
-            u = t - 1
-            ka, va, kready, vready = block(js[u])
-            g.tensor.wait_ge(sem["rd%d" % u], 1)
+        else:
+            g.tensor.wait_ge(sem["rd%d" % t], 1)
             if vready != kready:
                 g.tensor.wait_ge(sem[vready[0]], vready[1])
-            mm = g.tensor.matmul(T.pown[:, 0:128], va, T.ssb[:, u * 128:u * 128 + 128], u == 0, u == n - 1)
-            if u == n - 1:
+            mm = g.tensor.matmul(T.pown[:, 0:128], va, T.ssb[:, t * 128:t * 128 + 128], t == 0, t == n - 1)
+            if t == n - 1:
                 mm.then_inc(sem.owd, 1)
 
     g.vector.memset(T.zero[:, :], 0.0).then_inc(sem.zs, 1)

@@ -2,7 +2,7 @@ from concourse.bass import DstId, RemoteDMATransfer
 from concourse.mybir import AluOpType
 
 ROUTE = {(0, 1): "Y", (0, 3): "X", (1, 2): "X", (2, 3): "Y"}
-NB = 4
+NB = 7
 
 SCRATCH = {
     "dk": ("dram", [128, 128], "bfloat16"),
@@ -17,6 +17,9 @@ SCRATCH = {
     "ps1": ("psum", [128, 512], "float32"),
     "ps2": ("psum", [128, 512], "float32"),
     "ps3": ("psum", [128, 512], "float32"),
+    "ps4": ("psum", [128, 512], "float32"),
+    "ps5": ("psum", [128, 512], "float32"),
+    "ps6": ("psum", [128, 512], "float32"),
     "pown": ("psum", [128, 512], "float32"),
 }
 SEMAPHORES = (["ld_d", "ld_kv", "ld_q", "harr", "harv", "sent", "zs", "owd", "yd", "st"]
@@ -83,16 +86,15 @@ def rank_program(g, core, T, topo):
     g.scalar.dma_start(T.kv[:, 128:256], T.v[:, :]).then_inc(sem.ld_kv, 16)
     g.sync.dma_start(T.qs[:, :], T.q[:, :]).then_inc(sem.ld_q, 16)
 
-    early = [r] + ([r - 1] if par else [])
-    if c >= 2:
-        early += [2 * (c - 2), 2 * (c - 2) + 1]
+    home = [r] + ([r - 1] if par else [])
     late = []
     if c >= 1:
         late += [2 * (c - 1), 2 * (c - 1) + 1]
     if c == 3:
         late += [0, 1]
-    js = early + late
-    n, ne = len(js), len(early)
+    mid = [2 * (c - 2), 2 * (c - 2) + 1] if c >= 2 else []
+    js = home + late + mid
+    n, nh, nl = len(js), len(home), len(late)
 
     def block(j):
         if j == r:
@@ -128,15 +130,13 @@ def rank_program(g, core, T, topo):
     if nsent:
         g.wait_ge(sem.sent, nsent)
 
-    order = []
-    for t in range(ne):
-        order.append(("S", t))
-        if t > 0:
-            order.append(("O", t - 1))
+    order = [("S", t) for t in range(nh)] + [("O", t) for t in range(nh - 1)]
     if late:
-        order.append(("S", ne))
-    order.append(("O", ne - 1))
-    order += [("S", t) for t in range(ne + 1, n)] + [("O", t) for t in range(ne, n)]
+        order.append(("S", nh))
+    order.append(("O", nh - 1))
+    order += [("S", t) for t in range(nh + 1, n)]
+    order += [("O", t) for t in range(nh + nl, n)] + [("O", t) for t in range(nh, nh + nl)]
+    olast = order[-1][1]
     g.tensor.wait_ge(sem.ld_q, 16)
     for (op, t) in order:
         ka, va, kready, vready = block(js[t])
@@ -147,8 +147,8 @@ def rank_program(g, core, T, topo):
             g.tensor.wait_ge(sem["rd%d" % t], 1)
             if vready != kready:
                 g.tensor.wait_ge(sem[vready[0]], vready[1])
-            mm = g.tensor.matmul(T.pown[:, 0:128], va, T.ssb[:, t * 128:t * 128 + 128], t == 0, t == n - 1)
-            if t == n - 1:
+            mm = g.tensor.matmul(T.pown[:, 0:128], va, T.ssb[:, t * 128:t * 128 + 128], t == 0, t == olast)
+            if t == olast:
                 mm.then_inc(sem.owd, 1)
 
     g.vector.memset(T.zero[:, :], 0.0).then_inc(sem.zs, 1)

from concourse.bass import DstId, RemoteDMATransfer
from concourse.mybir import AluOpType

ROUTE = {(0, 1): "Y", (0, 3): "X", (1, 2): "X", (2, 3): "Y"}
NB = 7

SCRATCH = {
    "dk": ("dram", [128, 128], "bfloat16"),
    "dv": ("dram", [128, 128], "bfloat16"),
    "kv": ("sbuf", [128, 256], "bfloat16"),
    "qs": ("sbuf", [128, 128], "bfloat16"),
    "land": ("sbuf", [128, 7 * 256], "bfloat16"),
    "zero": ("sbuf", [128, 128], "float32"),
    "ssb": ("sbuf", [128, 1024], "bfloat16"),
    "ysb": ("sbuf", [128, 128], "bfloat16"),
    "ps0": ("psum", [128, 512], "float32"),
    "ps1": ("psum", [128, 512], "float32"),
    "ps2": ("psum", [128, 512], "float32"),
    "ps3": ("psum", [128, 512], "float32"),
    "ps4": ("psum", [128, 512], "float32"),
    "ps5": ("psum", [128, 512], "float32"),
    "ps6": ("psum", [128, 512], "float32"),
    "pown": ("psum", [128, 512], "float32"),
}
SEMAPHORES = (["ld_d", "ld_kv", "ld_q", "harr", "harv", "sent", "zs", "owd", "yd", "st"]
              + ["ka%d" % i for i in range(7)] + ["va%d" % i for i in range(7)]
              + ["sd%d" % i for i in range(8)] + ["rd%d" % i for i in range(8)])


def _routes(j, cores):
    cj = j // 2
    pair = 2 if j % 2 == 0 else 6
    cross, same = [], None
    for cd in range(cj + 1, 4):
        there = cores[2 * cd] - cores[2 * cd] % 8
        if (cd - cj) % 2 == 0:
            same = (there + pair, cd)
        elif ROUTE[(cj, cd)] == "X":
            cross.append((cores[j] - cores[j] % 8 + pair, cd, 8))
        else:
            cross.append(((there ^ 8) + pair, cd, 0))
    return cross, same


def _one(topo, core, d, mask, rsem, src, dst):
    rid, pid = topo.addr(d, core)
    return RemoteDMATransfer(dst_ids=[DstId(rid=rid, pnc=pid)], dma_engine_mask=mask, remote_sem=rsem, src=src, dst=dst)


def rank_program(g, core, T, topo):
    cores = T.cores
    sem = T.sem
    r = T.rank_of(core)

    if r is None:
        for j in range(6):
            cross, same = _routes(j, cores)
            for (h, cd, lo) in cross:
                if core in (h, h + 1):
                    rid, pid = topo.addr(cores[2 * cd + core - h], core)
                    g.wait_ge(sem.harr, 4)
                    g.remote_dma(out_ap=T.land[:, j * 256:j * 256 + 128], in_ap=T.dk[:, :], remote_sem=sem["ka%d" % j],
                                 local_sem=sem.sent, pid=pid, routing_id=rid, dma_engine_mask=0x00FF)
                    g.wait_ge(sem.harv, 4)
                    g.remote_dma(out_ap=T.land[:, j * 256 + 128:j * 256 + 256], in_ap=T.dv[:, :],
                                 remote_sem=sem["va%d" % j], local_sem=sem.sent, pid=pid, routing_id=rid,
                                 dma_engine_mask=0x00FF)
                    g.wait_ge(sem.sent, 16)
            if same is not None and core in (same[0], same[0] + 1):
                half = core - same[0]
                c0 = j * 256 + half * 128
                trs = [_one(topo, core, cores[2 * same[1] + i], 0xFF << (8 * i), sem[("va%d" if half else "ka%d") % j],
                            T.dk[:, :], T.land[:, c0:c0 + 128]) for i in range(2)]
                g.wait_ge(sem.harr, 4)
                g.remote_dma_fused(trs, local_sem=sem.sent)
                g.wait_ge(sem.sent, 16)
        return

    c, par = r // 2, r % 2
    cross, same = _routes(r, cores)

    if cross:
        g.sync.dma_start(T.dk[:, :], T.k[:, :]).then_inc(sem.ld_d, 16)
        g.scalar.dma_start(T.dv[:, :], T.v[:, :]).then_inc(sem.ld_d, 16)
    g.sync.dma_start(T.kv[:, 0:128], T.k[:, :]).then_inc(sem.ld_kv, 16)
    g.scalar.dma_start(T.kv[:, 128:256], T.v[:, :]).then_inc(sem.ld_kv, 16)
    g.sync.dma_start(T.qs[:, :], T.q[:, :]).then_inc(sem.ld_q, 16)

    home = [r] + ([r - 1] if par else [])
    late = []
    if c >= 1:
        late += [2 * (c - 1), 2 * (c - 1) + 1]
    if c == 3:
        late += [0, 1]
    mid = [2 * (c - 2), 2 * (c - 2) + 1] if c >= 2 else []
    js = home + late + mid
    n, nh, nl = len(js), len(home), len(late)

    def block(j):
        if j == r:
            return T.kv[:, 0:128], T.kv[:, 128:256], ("ld_kv", 32), ("ld_kv", 32)
        ka, va = T.land[:, j * 256:j * 256 + 128], T.land[:, j * 256 + 128:j * 256 + 256]
        if j // 2 == c:
            return ka, va, ("ka%d" % j, 16), ("ka%d" % j, 16)
        return ka, va, ("ka%d" % j, 8), ("va%d" % j, 8)

    nsent = 0
    if cross:
        kcall = [_one(topo, core, h + i, 0xF << (lo + 4 * i), sem.harr, T.dk[:, :], T.dk[:, :])
                 for (h, cd, lo) in cross for i in range(2)]
        vcall = [_one(topo, core, h + i, 0xF << (lo + 4 * i), sem.harv, T.dv[:, :], T.dv[:, :])
                 for (h, cd, lo) in cross for i in range(2)]
        scall = []
        if same is not None:
            scall = [_one(topo, core, same[0], 0x000F, sem.harr, T.dk[:, :], T.dk[:, :]),
                     _one(topo, core, same[0] + 1, 0x00F0, sem.harr, T.dv[:, :], T.dk[:, :])]
        if scall and all(lo == 8 for (h, cd, lo) in cross):
            kcall, scall = kcall + scall, []
        g.wait_ge(sem.ld_d, 32)
        for call in (kcall, scall, vcall):
            if call:
                g.remote_dma_fused(call, local_sem=sem.sent)
                nsent += 4 * len(call)
    if par == 0:
        rid, pid = topo.addr(cores[r + 1], core)
        g.wait_ge(sem.ld_kv, 32)
        g.remote_dma(out_ap=T.land[:, r * 256:r * 256 + 256], in_ap=T.kv[:, :], remote_sem=sem["ka%d" % r],
                     local_sem=sem.sent, pid=pid, routing_id=rid, dma_engine_mask=0xFFFF)
        nsent += 16
    if nsent:
        g.wait_ge(sem.sent, nsent)

    order = [("S", t) for t in range(nh)] + [("O", t) for t in range(nh - 1)]
    if late:
        order.append(("S", nh))
    order.append(("O", nh - 1))
    order += [("S", t) for t in range(nh + 1, n)]
    order += [("O", t) for t in range(nh + nl, n)] + [("O", t) for t in range(nh, nh + nl)]
    olast = order[-1][1]
    g.tensor.wait_ge(sem.ld_q, 16)
    for (op, t) in order:
        ka, va, kready, vready = block(js[t])
        if op == "S":
            g.tensor.wait_ge(sem[kready[0]], kready[1])
            g.tensor.matmul(T["ps%d" % (t % NB)][:, 0:128], ka, T.qs[:, :], True, True).then_inc(sem["sd%d" % t], 1)
        else:
            g.tensor.wait_ge(sem["rd%d" % t], 1)
            if vready != kready:
                g.tensor.wait_ge(sem[vready[0]], vready[1])
            mm = g.tensor.matmul(T.pown[:, 0:128], va, T.ssb[:, t * 128:t * 128 + 128], t == 0, t == olast)
            if t == olast:
                mm.then_inc(sem.owd, 1)

    g.vector.memset(T.zero[:, :], 0.0).then_inc(sem.zs, 1)
    g.vector.wait_ge(sem.zs, 1)
    for t in range(n):
        g.vector.wait_ge(sem["sd%d" % t], 1)
        g.vector.tensor_tensor(T.ssb[:, t * 128:t * 128 + 128], T["ps%d" % (t % NB)][:, 0:128], T.zero[:, :],
                               AluOpType.max).then_inc(sem["rd%d" % t], 1)
    g.vector.wait_ge(sem.owd, 1)
    g.vector.tensor_copy(T.ysb[:, :], T.pown[:, 0:128]).then_inc(sem.yd, 1)

    g.sync.wait_ge(sem.yd, 1)
    g.sync.dma_start(T.y[:, :], T.ysb[:, :]).then_inc(sem.st, 16)
    g.sync.wait_ge(sem.st, 16)
